import numpy as np
import ml_dtypes


def mxq(x, axis, fmt="e4m3"):
    dtype, down = {"e4m3": (ml_dtypes.float8_e4m3fn, 7), "e5m2": (ml_dtypes.float8_e5m2, 14)}[fmt]
    v = np.moveaxis(np.asarray(x, np.float32).astype(ml_dtypes.bfloat16).astype(np.float64), axis, -1)
    blocks = v.reshape(v.shape[:-1] + (-1, 32))
    amax = np.abs(blocks).max(-1, keepdims=True)
    byte = np.maximum(np.where(amax > 0, np.frexp(amax)[1] - 1 + 127, 0) - down, 1)
    scale = np.exp2(byte - 127.0)
    codes = (blocks / scale).astype(np.float32).astype(dtype).astype(np.float64)
    return np.moveaxis((codes * scale).reshape(v.shape), -1, axis)


WIDE = False


def mx_kscale(k):
    if not WIDE:
        return np.ones(k)
    levels = np.array([10, -10, 5, -5, 0])
    if k % 512:
        return np.exp2(np.random.permutation(np.resize(levels, k // 32))).repeat(32)
    a = np.empty((k // 512, 16))
    for p in range(k // 512):
        a[p, :8] = np.random.permutation(np.resize(levels, 8))
        for g in range(8):
            far = levels[np.abs(levels - a[p, g]) >= 10]
            a[p, g + 8] = far[np.random.randint(len(far))]
    return np.exp2(a.ravel()).repeat(32)


BF16 = ml_dtypes.bfloat16


def bf(x):
    return np.asarray(x, np.float32).astype(BF16)


def f64(x):
    return np.asarray(x).astype(np.float64)

E4M3FN = np.array([(-1.0 if i & 128 else 1.0) * ((1.0 + (i & 7) / 8.0) * 2.0 ** (((i >> 3) & 15) - 7) if i & 120 else (i & 7) * 2.0 ** -9) for i in range(256)])


def e4m3fn_bytes(y):
    return np.clip(np.asarray(y, np.float64), -448.0, 448.0).astype(np.float32).astype(ml_dtypes.float8_e4m3fn).view(np.uint8)


def e4m3fn_values(b):
    return E4M3FN[b]

def planes(Y):
    n, m = Y.shape
    b = f64(bf(Y)).reshape(n // 32, 32, m)
    amax = np.abs(b).max(1)
    byte = np.clip(np.where(amax > 0, np.frexp(amax)[1] - 1 + 127 - 7, 1), 1, 254)
    codes = (b * np.exp2(127.0 - byte)[:, None, :]).reshape(n, m).astype(np.float32).astype(ml_dtypes.float8_e4m3fn).view(np.uint8)
    words = codes.reshape(n // 512, 128, 4, m).transpose(0, 1, 3, 2)
    return np.ascontiguousarray(words), np.ascontiguousarray(byte.astype(np.uint8).reshape(n // 512, 16, m))


S, F, N = 2048, 1024, 1536
MU = 0.6
FP8_MAX = 448.0


def setup_inputs():
    s = mx_kscale(S)[:, None]
    X = np.random.randn(S, F) * np.exp(0.3 * np.random.randn(S, 1)) * s
    D = np.random.randn(S, N) * np.exp(0.3 * np.random.randn(S, 1)) * (2.0 / np.sqrt(S)) / s
    X_scale = (np.abs(X).max(axis=1, keepdims=True) / FP8_MAX).astype(np.float32)
    D_scale = (np.abs(D).max(axis=1, keepdims=True) / FP8_MAX).astype(np.float32)
    X_bytes = e4m3fn_bytes(X / f64(X_scale))
    D_bytes = e4m3fn_bytes(D / f64(D_scale))
    spread = np.exp(0.8 * np.random.randn(F, 1))
    W = 0.6 * np.random.randn(F, N) * spread
    eta = 0.8 * spread * np.exp(0.1 * np.random.randn(F, 1))
    V = np.random.randn(F, N)
    return {"X_bytes": X_bytes, "X_scale": X_scale,
            "D_bytes": D_bytes, "D_scale": D_scale,
            "V": bf(V), "W": bf(W), "eta": bf(eta)}


def reference(X_bytes, X_scale, D_bytes, D_scale, V, W, eta):
    X = e4m3fn_values(X_bytes) * f64(X_scale)
    D = e4m3fn_values(D_bytes) * f64(D_scale)
    G = mxq(X, 0, "e4m3").T @ mxq(D, 0, "e4m3")
    A = MU * f64(V) + (1.0 - MU) * G
    y = f64(W) - f64(eta) * np.tanh(A)
    words, scales = planes(y)
    return y, words, scales

@@ -1,0 +1,241 @@
+from contextlib import ExitStack
+
+import concourse.mybir as mybir
+
+S, F, N = 2048, 1024, 1536
+MU = 0.6
+FLOPS = 2 * S * F * N
+
+F32 = mybir.dt.float32
+BF16 = mybir.dt.bfloat16
+I32 = mybir.dt.int32
+U32 = mybir.dt.uint32
+U8 = mybir.dt.uint8
+FP8 = mybir.dt.float8_e4m3fn
+FP8X4 = mybir.dt.float8_e4m3fn_x4
+ACT = mybir.ActivationFunctionType
+ALU = mybir.AluOpType
+
+P = 128
+PACK = 4
+K_PASS = P * PACK
+PASSES = S // K_PASS
+PIECE = 512
+UNIT = 256
+GROUPS = F // K_PASS
+CHUNKS = N // PIECE
+FIRST_UNIT_STEP = 14
+OPEN_UNITS = 4
+
+
+def tile_fp8_wgrad_momentum_tanh_b3_kernel(
+    tc, X_bytes, X_scale, D_bytes, D_scale, V, W, eta, out_0, out_1, out_2
+):
+    nc = tc.nc
+    pieces = []
+    for k in range(PASSES):
+        pieces.extend([("d", 0, k), ("x", 0, k), ("x", 1, k)])
+    for c in range(1, CHUNKS):
+        pieces.extend([("d", c, k) for k in range(PASSES)])
+    units = [(g, h) for h in range(N // UNIT) for g in range(GROUPS)]
+    on_vector = {(0, 0), (0, 1), (1, 0), (1, 1)} | {(i, 0) for i in range(3, 12, 2)}
+
+    with ExitStack() as ctx:
+        keep = ctx.enter_context(tc.tile_pool(name="keep", bufs=1))
+        work = ctx.enter_context(tc.tile_pool(name="work", bufs=3))
+        outs = ctx.enter_context(tc.tile_pool(name="outs", bufs=4))
+        psum = ctx.enter_context(tc.psum_pool(name="psum", bufs=2 * OPEN_UNITS))
+        ctx.enter_context(tc.manual_schedule())
+
+        token_scale = {}
+        for name, src in (("d", D_scale), ("x", X_scale)):
+            token_scale[name] = keep.tile([P, PASSES, PACK], F32, name="scale_" + name)
+            nc.scalar.dma_start(
+                out=token_scale[name][:],
+                in_=src.rearrange("(k p t) o -> p k (t o)", p=P, t=PACK),
+            )
+        warm_in = keep.tile([P, 1], F32, name="warm_in")
+        warm_out = keep.tile([P, 1], F32, name="warm_out")
+        nc.gpsimd.memset(warm_in[:], 0.0)
+        nc.scalar.activation(out=warm_out[:], in_=warm_in[:], func=ACT.Tanh)
+
+        x_rows = X_bytes.rearrange("(k p t) f -> k p t f", p=P, t=PACK)
+        d_rows = D_bytes.rearrange("(k p t) n -> k p t n", p=P, t=PACK)
+        raw = {}
+        for k in range(PASSES):
+            d_first = keep.tile([P, PACK, PIECE], U8, name="d_first_%d" % k)
+            nc.sync.dma_start(out=d_first[:], in_=d_rows[k][:, :, 0:PIECE])
+            raw[("d", 0, k)] = d_first[:]
+            x_pass = keep.tile([P, PACK, F], U8, name="x_pass_%d" % k)
+            nc.sync.dma_start(out=x_pass[:], in_=x_rows[k])
+            for g in range(GROUPS):
+                raw[("x", g, k)] = x_pass[:, :, g * PIECE : (g + 1) * PIECE]
+        for k in range(PASSES):
+            d_rest = keep.tile([P, PACK, N - PIECE], U8, name="d_rest_%d" % k)
+            nc.sync.dma_start(out=d_rest[:], in_=d_rows[k][:, :, PIECE:N])
+            for c in range(1, CHUNKS):
+                raw[("d", c, k)] = d_rest[:, :, (c - 1) * PIECE : c * PIECE]
+        step_size = keep.tile([P, GROUPS, PACK], BF16, name="step_size")
+        nc.sync.dma_start(
+            out=step_size[:], in_=eta.rearrange("(g p t) o -> p g (t o)", p=P, t=PACK)
+        )
+        old = {}
+        for name, src in (("v", V), ("w", W)):
+            rows = src.rearrange("(g p t) n -> g p t n", p=P, t=PACK)
+            for g in range(GROUPS):
+                old[(name, g)] = keep.tile([P, PACK, N], BF16, name="old_%s_%d" % (name, g))
+                nc.sync.dma_start(out=old[(name, g)][:], in_=rows[g])
+
+        y_rows = out_0.rearrange("(g p t) n -> g p t n", p=P, t=PACK)
+        y_words = out_1.rearrange("g p n t -> g p (n t)").bitcast(I32)
+        y_scales = out_2.bitcast(I32)
+        scale_out = [
+            keep.tile([P, N], U8, name="scale_out_%d" % g, align_bytes=64) for g in range(GROUPS)
+        ]
+
+        planes, mixed, codes, scales = {}, {}, {}, {}
+        banks, average, bounded, updated, rounded = {}, {}, {}, {}, {}
+
+        def widen(i, vector_part):
+            name, c, k = pieces[i]
+            if i not in planes:
+                planes[i] = work.tile([P, PACK, PIECE], BF16, name="planes")
+            for t in range(PACK):
+                if ((i, t) in on_vector) != vector_part:
+                    continue
+                src = raw[pieces[i]][:, t, :].bitcast(FP8)
+                col = token_scale[name][:, k, t : t + 1]
+                if vector_part:
+                    nc.vector.tensor_scalar(
+                        out=planes[i][:, t, :], in0=src, scalar1=col, scalar2=None, op0=ALU.mult
+                    )
+                else:
+                    nc.scalar.activation(out=planes[i][:, t, :], in_=src, func=ACT.Copy, scale=col)
+
+        def interleave(i):
+            mixed[i] = work.tile([P, PIECE * PACK], BF16, name="mixed", align_bytes=64)
+            if pieces[i][0] == "x":
+                dst = mixed[i][:].rearrange("p (r a e t) -> p a r e t", r=PACK, e=2, t=PACK)
+                src = planes[i][:].rearrange("p t (a e r) -> p a r e t", e=2, r=PACK)
+            else:
+                dst = mixed[i][:].rearrange("p (a e t) -> p a t e", e=4, t=PACK)
+                src = planes[i][:].rearrange("p t (a e) -> p a t e", e=4)
+            nc.vector.tensor_copy(out=dst, in_=src)
+
+        def quantize(i):
+            codes[pieces[i]] = keep.tile([P, PIECE], U32, name="codes_%d" % i, align_bytes=64)
+            scales[pieces[i]] = keep.tile([P, PIECE], U8, name="scales_%d" % i, align_bytes=64)
+            nc.vector.quantize_mx(
+                out=codes[pieces[i]][:].bitcast(FP8X4), scales=scales[pieces[i]][:], in_=mixed[i][:]
+            )
+
+        def multiply(u):
+            g, h = units[u]
+            c, half = divmod(h, PIECE // UNIT)
+            n_cols = slice(half * UNIT, (half + 1) * UNIT)
+            banks[u] = []
+            for b in range(2):
+                bank = psum.tile([P, 2, UNIT], F32, name="bank")
+                banks[u].append(bank)
+                for j in range(2):
+                    r = 2 * b + j
+                    m_cols = slice(r * P, (r + 1) * P)
+                    for k in range(PASSES):
+                        nc.tensor.matmul_mx(
+                            out=bank[:, j, :],
+                            lhsT=codes[("x", g, k)][:, m_cols].bitcast(FP8X4),
+                            lhsT_scale=scales[("x", g, k)][:, m_cols],
+                            rhs=codes[("d", c, k)][:, n_cols].bitcast(FP8X4),
+                            rhs_scale=scales[("d", c, k)][:, n_cols],
+                            start=(k == 0),
+                            stop=(k == PASSES - 1),
+                        )
+
+        def multiply_ready():
+            for u in range(len(banks), len(units)):
+                g, h = units[u]
+                needs = [("x", g, PASSES - 1), ("d", h * UNIT // PIECE, PASSES - 1)]
+                if not all(n in codes for n in needs):
+                    break
+                if u >= OPEN_UNITS and u - OPEN_UNITS not in average:
+                    break
+                multiply(u)
+
+        def momentum(u):
+            g, h = units[u]
+            cols = slice(h * UNIT, (h + 1) * UNIT)
+            average[u] = work.tile([P, PACK, UNIT], F32, name="average")
+            for b in range(2):
+                nc.vector.scalar_tensor_tensor(
+                    out=average[u][:, 2 * b : 2 * b + 2, :],
+                    in0=old[("v", g)][:, 2 * b : 2 * b + 2, cols],
+                    scalar=MU / (1.0 - MU),
+                    in1=banks[u][b][:],
+                    op0=ALU.mult,
+                    op1=ALU.add,
+                )
+
+        def bound(u):
+            bounded[u] = work.tile([P, PACK, UNIT], F32, name="bounded")
+            nc.scalar.activation(
+                out=bounded[u][:], in_=average[u][:], func=ACT.Tanh, scale=-(1.0 - MU)
+            )
+
+        def update(u):
+            g, h = units[u]
+            cols = slice(h * UNIT, (h + 1) * UNIT)
+            updated[u] = outs.tile([P, PACK, UNIT], F32, name="updated")
+            for r in range(PACK):
+                nc.vector.scalar_tensor_tensor(
+                    out=updated[u][:, r, :],
+                    in0=bounded[u][:, r, :],
+                    scalar=step_size[:, g, r : r + 1],
+                    in1=old[("w", g)][:, r, cols],
+                    op0=ALU.mult,
+                    op1=ALU.add,
+                )
+            nc.sync.dma_start(out=y_rows[g][:, :, cols], in_=updated[u][:])
+
+        def round_y(u):
+            rounded[u] = work.tile([P, UNIT * PACK], BF16, name="rounded", align_bytes=64)
+            nc.scalar.copy(
+                out=rounded[u][:].rearrange("p (a e r) -> p a r e", e=4, r=PACK),
+                in_=updated[u][:].rearrange("p r (a e) -> p a r e", e=4),
+            )
+
+        def quantize_y(u):
+            g, h = units[u]
+            cols = slice(h * UNIT, (h + 1) * UNIT)
+            words = outs.tile([P, UNIT], U32, name="words_out", align_bytes=64)
+            nc.vector.quantize_mx(
+                out=words[:].bitcast(FP8X4), scales=scale_out[g][:, cols], in_=rounded[u][:]
+            )
+            nc.sync.dma_start(out=y_words[g][:, cols], in_=words[:].bitcast(I32))
+            if h == N // UNIT - 1:
+                for q in range(4):
+                    nc.sync.dma_start(
+                        out=y_scales[g][4 * q : 4 * q + 4, :],
+                        in_=scale_out[g][32 * q : 32 * q + 4, :].bitcast(I32),
+                    )
+
+        def piece_stage(stage, i, *more):
+            if 0 <= i < len(pieces):
+                stage(i, *more)
+
+        def unit_stage(stage, u):
+            if 0 <= u < len(units):
+                stage(u)
+
+        for step in range(-1, FIRST_UNIT_STEP + len(units) + 4):
+            u = step - FIRST_UNIT_STEP
+            unit_stage(momentum, u)
+            multiply_ready()
+            piece_stage(widen, step + 1, True)
+            piece_stage(interleave, step)
+            unit_stage(update, u - 2)
+            unit_stage(quantize_y, u - 4)
+            piece_stage(quantize, step - 1)
+            multiply_ready()
+            unit_stage(bound, u - 1)
+            unit_stage(round_y, u - 3)
+            piece_stage(widen, step + 1, False)

@@ -115,12 +115,15 @@ def tile_fp8_wgrad_momentum_tanh_b3_kernel(
         def interleave(i):
             mixed[i] = work.tile([P, PIECE * PACK], BF16, name="mixed", align_bytes=64)
             if pieces[i][0] == "x":
-                dst = mixed[i][:].rearrange("p (r a e t) -> p a r e t", r=PACK, e=2, t=PACK)
-                src = planes[i][:].rearrange("p t (a e r) -> p a r e t", e=2, r=PACK)
+                dst = mixed[i][:].rearrange("p (r a e t) -> p a t e r", r=PACK, e=2, t=PACK)
+                src = planes[i][:].rearrange("p t (a e r) -> p a t e r", e=2, r=PACK)
             else:
                 dst = mixed[i][:].rearrange("p (a e t) -> p a t e", e=4, t=PACK)
                 src = planes[i][:].rearrange("p t (a e) -> p a t e", e=4)
-            nc.vector.tensor_copy(out=dst, in_=src)
+            if i == len(pieces) - 1:
+                nc.scalar.copy(out=dst, in_=src)
+            else:
+                nc.vector.tensor_copy(out=dst, in_=src)
 
         def quantize(i):
             codes[pieces[i]] = keep.tile([P, PIECE], U32, name="codes_%d" % i, align_bytes=64)
@@ -198,10 +201,12 @@ def tile_fp8_wgrad_momentum_tanh_b3_kernel(
 
         def round_y(u):
             rounded[u] = work.tile([P, UNIT * PACK], BF16, name="rounded", align_bytes=64)
-            nc.scalar.copy(
-                out=rounded[u][:].rearrange("p (a e r) -> p a r e", e=4, r=PACK),
-                in_=updated[u][:].rearrange("p r (a e) -> p a r e", e=4),
-            )
+            dst = rounded[u][:].rearrange("p (a e r) -> p a r e", e=4, r=PACK)
+            src = updated[u][:].rearrange("p r (a e) -> p a r e", e=4)
+            if u == len(units) - 1:
+                nc.vector.tensor_copy(out=dst, in_=src)
+            else:
+                nc.scalar.copy(out=dst, in_=src)
 
         def quantize_y(u):
             g, h = units[u]
@@ -213,7 +218,7 @@ def tile_fp8_wgrad_momentum_tanh_b3_kernel(
             nc.sync.dma_start(out=y_words[g][:, cols], in_=words[:].bitcast(I32))
             if h == N // UNIT - 1:
                 for q in range(4):
-                    nc.sync.dma_start(
+                    nc.scalar.dma_start(
                         out=y_scales[g][4 * q : 4 * q + 4, :],
                         in_=scale_out[g][32 * q : 32 * q + 4, :].bitcast(I32),
                     )
@@ -231,11 +236,17 @@ def tile_fp8_wgrad_momentum_tanh_b3_kernel(
             unit_stage(momentum, u)
             multiply_ready()
             piece_stage(widen, step + 1, True)
-            piece_stage(interleave, step)
+            if step != len(pieces) - 1:
+                piece_stage(interleave, step)
             unit_stage(update, u - 2)
+            if u - 3 == len(units) - 1:
+                round_y(u - 3)
             unit_stage(quantize_y, u - 4)
             piece_stage(quantize, step - 1)
             multiply_ready()
             unit_stage(bound, u - 1)
-            unit_stage(round_y, u - 3)
+            if u - 3 != len(units) - 1:
+                unit_stage(round_y, u - 3)
+            if step == len(pieces) - 1:
+                interleave(step)
             piece_stage(widen, step + 1, False)

@@ -37,13 +37,13 @@ def tile_fp8_wgrad_momentum_tanh_b3_kernel(
         pieces.extend([("d", 0, k), ("x", 0, k), ("x", 1, k)])
     for c in range(1, CHUNKS):
         pieces.extend([("d", c, k) for k in range(PASSES)])
-    units = [(g, h) for h in range(N // UNIT) for g in range(GROUPS)]
+    units = [(g, c, b) for c in range(CHUNKS) for g in range(GROUPS) for b in range(2)]
     on_vector = {(0, 0), (0, 1), (1, 0), (1, 1)} | {(i, 0) for i in range(3, 12, 2)}
 
     with ExitStack() as ctx:
         keep = ctx.enter_context(tc.tile_pool(name="keep", bufs=1))
         work = ctx.enter_context(tc.tile_pool(name="work", bufs=3))
-        outs = ctx.enter_context(tc.tile_pool(name="outs", bufs=4))
+        outs = ctx.enter_context(tc.tile_pool(name="outs", bufs=3))
         psum = ctx.enter_context(tc.psum_pool(name="psum", bufs=2 * OPEN_UNITS))
         ctx.enter_context(tc.manual_schedule())
 
@@ -64,7 +64,8 @@ def tile_fp8_wgrad_momentum_tanh_b3_kernel(
         raw = {}
         for k in range(PASSES):
             d_first = keep.tile([P, PACK, PIECE], U8, name="d_first_%d" % k)
-            nc.sync.dma_start(out=d_first[:], in_=d_rows[k][:, :, 0:PIECE])
+            for rows in [slice(0, 2), slice(2, 4)] if k == 0 else [slice(0, 4)]:
+                nc.sync.dma_start(out=d_first[:, rows, :], in_=d_rows[k][:, rows, 0:PIECE])
             raw[("d", 0, k)] = d_first[:]
             x_pass = keep.tile([P, PACK, F], U8, name="x_pass_%d" % k)
             nc.sync.dma_start(out=x_pass[:], in_=x_rows[k])
@@ -89,12 +90,11 @@ def tile_fp8_wgrad_momentum_tanh_b3_kernel(
         y_rows = out_0.rearrange("(g p t) n -> g p t n", p=P, t=PACK)
         y_words = out_1.rearrange("g p n t -> g p (n t)").bitcast(I32)
         y_scales = out_2.bitcast(I32)
-        scale_out = [
-            keep.tile([P, N], U8, name="scale_out_%d" % g, align_bytes=64) for g in range(GROUPS)
-        ]
+        scale_out = keep.tile([P, N], U8, name="scale_out", align_bytes=64)
 
         planes, mixed, codes, scales = {}, {}, {}, {}
-        banks, average, bounded, updated, rounded = {}, {}, {}, {}, {}
+        banks, average, bounded, updated, rounded, words = {}, {}, {}, {}, {}, {}
+        passes_done = {u: 0 for u in range(len(units))}
 
         def widen(i, vector_part):
             name, c, k = pieces[i]
@@ -132,95 +132,99 @@ def tile_fp8_wgrad_momentum_tanh_b3_kernel(
                 out=codes[pieces[i]][:].bitcast(FP8X4), scales=scales[pieces[i]][:], in_=mixed[i][:]
             )
 
-        def multiply(u):
-            g, h = units[u]
-            c, half = divmod(h, PIECE // UNIT)
-            n_cols = slice(half * UNIT, (half + 1) * UNIT)
-            banks[u] = []
-            for b in range(2):
-                bank = psum.tile([P, 2, UNIT], F32, name="bank")
-                banks[u].append(bank)
-                for j in range(2):
-                    r = 2 * b + j
-                    m_cols = slice(r * P, (r + 1) * P)
-                    for k in range(PASSES):
+        def multiply_ready():
+            for k in range(PASSES):
+                for u, (g, c, b) in enumerate(units):
+                    if passes_done[u] != k or (u >= OPEN_UNITS and u - OPEN_UNITS not in average):
+                        continue
+                    if ("x", g, k) not in codes or ("d", c, k) not in codes:
+                        continue
+                    for j in range(2):
+                        if k == 0:
+                            banks[(u, j)] = psum.tile([P, PIECE], F32, name="bank")
+                        r = 2 * b + j
+                        m_cols = slice(r * P, (r + 1) * P)
                         nc.tensor.matmul_mx(
-                            out=bank[:, j, :],
+                            out=banks[(u, j)][:],
                             lhsT=codes[("x", g, k)][:, m_cols].bitcast(FP8X4),
                             lhsT_scale=scales[("x", g, k)][:, m_cols],
-                            rhs=codes[("d", c, k)][:, n_cols].bitcast(FP8X4),
-                            rhs_scale=scales[("d", c, k)][:, n_cols],
+                            rhs=codes[("d", c, k)][:].bitcast(FP8X4),
+                            rhs_scale=scales[("d", c, k)][:],
                             start=(k == 0),
                             stop=(k == PASSES - 1),
                         )
-
-        def multiply_ready():
-            for u in range(len(banks), len(units)):
-                g, h = units[u]
-                needs = [("x", g, PASSES - 1), ("d", h * UNIT // PIECE, PASSES - 1)]
-                if not all(n in codes for n in needs):
-                    break
-                if u >= OPEN_UNITS and u - OPEN_UNITS not in average:
-                    break
-                multiply(u)
+                    passes_done[u] = k + 1
 
         def momentum(u):
-            g, h = units[u]
-            cols = slice(h * UNIT, (h + 1) * UNIT)
-            average[u] = work.tile([P, PACK, UNIT], F32, name="average")
-            for b in range(2):
+            g, c, b = units[u]
+            cols = slice(c * PIECE, (c + 1) * PIECE)
+            average[u] = work.tile([P, 2, PIECE], F32, name="average")
+            for j in range(2):
                 nc.vector.scalar_tensor_tensor(
-                    out=average[u][:, 2 * b : 2 * b + 2, :],
-                    in0=old[("v", g)][:, 2 * b : 2 * b + 2, cols],
+                    out=average[u][:, j, :],
+                    in0=old[("v", g)][:, 2 * b + j, cols],
                     scalar=MU / (1.0 - MU),
-                    in1=banks[u][b][:],
+                    in1=banks[(u, j)][:],
                     op0=ALU.mult,
                     op1=ALU.add,
                 )
 
         def bound(u):
-            bounded[u] = work.tile([P, PACK, UNIT], F32, name="bounded")
+            bounded[u] = work.tile([P, 2, PIECE], F32, name="bounded")
             nc.scalar.activation(
                 out=bounded[u][:], in_=average[u][:], func=ACT.Tanh, scale=-(1.0 - MU)
             )
 
         def update(u):
-            g, h = units[u]
-            cols = slice(h * UNIT, (h + 1) * UNIT)
-            updated[u] = outs.tile([P, PACK, UNIT], F32, name="updated")
-            for r in range(PACK):
+            g, c, b = units[u]
+            cols = slice(c * PIECE, (c + 1) * PIECE)
+            if b == 0:
+                updated[(g, c)] = work.tile([P, PACK, PIECE], F32, name="updated")
+            for j in range(2):
+                r = 2 * b + j
                 nc.vector.scalar_tensor_tensor(
-                    out=updated[u][:, r, :],
-                    in0=bounded[u][:, r, :],
+                    out=updated[(g, c)][:, r, :],
+                    in0=bounded[u][:, j, :],
                     scalar=step_size[:, g, r : r + 1],
                     in1=old[("w", g)][:, r, cols],
                     op0=ALU.mult,
                     op1=ALU.add,
                 )
-            nc.sync.dma_start(out=y_rows[g][:, :, cols], in_=updated[u][:])
+            nc.sync.dma_start(
+                out=y_rows[g][:, 2 * b : 2 * b + 2, cols],
+                in_=updated[(g, c)][:, 2 * b : 2 * b + 2, :],
+            )
 
         def round_y(u):
+            g, c, b = units[u]
             rounded[u] = work.tile([P, UNIT * PACK], BF16, name="rounded", align_bytes=64)
             dst = rounded[u][:].rearrange("p (a e r) -> p a r e", e=4, r=PACK)
-            src = updated[u][:].rearrange("p r (a e) -> p a r e", e=4)
-            if u == len(units) - 1:
+            src = updated[(g, c)][:, :, b * UNIT : (b + 1) * UNIT].rearrange("p r (a e) -> p a r e", e=4)
+            if u == len(units) - 2:
                 nc.vector.tensor_copy(out=dst, in_=src)
             else:
                 nc.scalar.copy(out=dst, in_=src)
 
         def quantize_y(u):
-            g, h = units[u]
-            cols = slice(h * UNIT, (h + 1) * UNIT)
-            words = outs.tile([P, UNIT], U32, name="words_out", align_bytes=64)
+            g, c, b = units[u]
+            cols = slice(c * PIECE + b * UNIT, c * PIECE + (b + 1) * UNIT)
+            if b == 0:
+                words[(g, c)] = outs.tile([P, PIECE], U32, name="words_out", align_bytes=64)
             nc.vector.quantize_mx(
-                out=words[:].bitcast(FP8X4), scales=scale_out[g][:, cols], in_=rounded[u][:]
+                out=words[(g, c)][:, b * UNIT : (b + 1) * UNIT].bitcast(FP8X4),
+                scales=scale_out[4 * g : P, cols],
+                in_=rounded[u][:],
             )
-            nc.sync.dma_start(out=y_words[g][:, cols], in_=words[:].bitcast(I32))
-            if h == N // UNIT - 1:
+            if b == 1:
+                nc.sync.dma_start(
+                    out=y_words[g][:, c * PIECE : (c + 1) * PIECE],
+                    in_=words[(g, c)][:].bitcast(I32),
+                )
+            if u == len(units) - 1:
                 for q in range(4):
                     nc.scalar.dma_start(
-                        out=y_scales[g][4 * q : 4 * q + 4, :],
-                        in_=scale_out[g][32 * q : 32 * q + 4, :].bitcast(I32),
+                        out=y_scales[:, 4 * q : 4 * q + 4, :],
+                        in_=scale_out[32 * q : 32 * q + 4 * GROUPS, :].bitcast(I32),
                     )
 
         def piece_stage(stage, i, *more):
@@ -231,7 +235,7 @@ def tile_fp8_wgrad_momentum_tanh_b3_kernel(
             if 0 <= u < len(units):
                 stage(u)
 
-        for step in range(-1, FIRST_UNIT_STEP + len(units) + 4):
+        for step in range(-1, FIRST_UNIT_STEP + len(units) + 5):
             u = step - FIRST_UNIT_STEP
             unit_stage(momentum, u)
             multiply_ready()
@@ -239,14 +243,14 @@ def tile_fp8_wgrad_momentum_tanh_b3_kernel(
             if step != len(pieces) - 1:
                 piece_stage(interleave, step)
             unit_stage(update, u - 2)
-            if u - 3 == len(units) - 1:
-                round_y(u - 3)
-            unit_stage(quantize_y, u - 4)
+            if u - 4 == len(units) - 2:
+                round_y(u - 4)
+            unit_stage(quantize_y, u - 5)
             piece_stage(quantize, step - 1)
             multiply_ready()
             unit_stage(bound, u - 1)
-            if u - 3 != len(units) - 1:
-                unit_stage(round_y, u - 3)
+            if u - 4 != len(units) - 2:
+                unit_stage(round_y, u - 4)
             if step == len(pieces) - 1:
                 interleave(step)
             piece_stage(widen, step + 1, False)

from contextlib import ExitStack

import concourse.mybir as mybir

S, F, N = 2048, 1024, 1536
MU = 0.6
FLOPS = 2 * S * F * N

F32 = mybir.dt.float32
BF16 = mybir.dt.bfloat16
I32 = mybir.dt.int32
U32 = mybir.dt.uint32
U8 = mybir.dt.uint8
FP8 = mybir.dt.float8_e4m3fn
FP8X4 = mybir.dt.float8_e4m3fn_x4
ACT = mybir.ActivationFunctionType
ALU = mybir.AluOpType

P = 128
PACK = 4
K_PASS = P * PACK
PASSES = S // K_PASS
PIECE = 512
UNIT = 256
GROUPS = F // K_PASS
CHUNKS = N // PIECE
FIRST_UNIT_STEP = 14
OPEN_UNITS = 4


def tile_fp8_wgrad_momentum_tanh_b3_kernel(
    tc, X_bytes, X_scale, D_bytes, D_scale, V, W, eta, out_0, out_1, out_2
):
    nc = tc.nc
    pieces = []
    for k in range(PASSES):
        pieces.extend([("d", 0, k), ("x", 0, k), ("x", 1, k)])
    for c in range(1, CHUNKS):
        pieces.extend([("d", c, k) for k in range(PASSES)])
    units = [(g, c, b) for c in range(CHUNKS) for g in range(GROUPS) for b in range(2)]
    on_vector = {(0, 0), (0, 1), (1, 0), (1, 1)} | {(i, 0) for i in range(3, 12, 2)}

    with ExitStack() as ctx:
        keep = ctx.enter_context(tc.tile_pool(name="keep", bufs=1))
        work = ctx.enter_context(tc.tile_pool(name="work", bufs=3))
        outs = ctx.enter_context(tc.tile_pool(name="outs", bufs=3))
        psum = ctx.enter_context(tc.psum_pool(name="psum", bufs=2 * OPEN_UNITS))
        ctx.enter_context(tc.manual_schedule())

        token_scale = {}
        for name, src in (("d", D_scale), ("x", X_scale)):
            token_scale[name] = keep.tile([P, PASSES, PACK], F32, name="scale_" + name)
            nc.scalar.dma_start(
                out=token_scale[name][:],
                in_=src.rearrange("(k p t) o -> p k (t o)", p=P, t=PACK),
            )
        warm_in = keep.tile([P, 1], F32, name="warm_in")
        warm_out = keep.tile([P, 1], F32, name="warm_out")
        nc.gpsimd.memset(warm_in[:], 0.0)
        nc.scalar.activation(out=warm_out[:], in_=warm_in[:], func=ACT.Tanh)

        x_rows = X_bytes.rearrange("(k p t) f -> k p t f", p=P, t=PACK)
        d_rows = D_bytes.rearrange("(k p t) n -> k p t n", p=P, t=PACK)
        raw = {}
        for k in range(PASSES):
            d_first = keep.tile([P, PACK, PIECE], U8, name="d_first_%d" % k)
            for rows in [slice(0, 2), slice(2, 4)] if k == 0 else [slice(0, 4)]:
                nc.sync.dma_start(out=d_first[:, rows, :], in_=d_rows[k][:, rows, 0:PIECE])
            raw[("d", 0, k)] = d_first[:]
            x_pass = keep.tile([P, PACK, F], U8, name="x_pass_%d" % k)
            nc.sync.dma_start(out=x_pass[:], in_=x_rows[k])
            for g in range(GROUPS):
                raw[("x", g, k)] = x_pass[:, :, g * PIECE : (g + 1) * PIECE]
        for k in range(PASSES):
            d_rest = keep.tile([P, PACK, N - PIECE], U8, name="d_rest_%d" % k)
            nc.sync.dma_start(out=d_rest[:], in_=d_rows[k][:, :, PIECE:N])
            for c in range(1, CHUNKS):
                raw[("d", c, k)] = d_rest[:, :, (c - 1) * PIECE : c * PIECE]
        step_size = keep.tile([P, GROUPS, PACK], BF16, name="step_size")
        nc.sync.dma_start(
            out=step_size[:], in_=eta.rearrange("(g p t) o -> p g (t o)", p=P, t=PACK)
        )
        old = {}
        for name, src in (("v", V), ("w", W)):
            rows = src.rearrange("(g p t) n -> g p t n", p=P, t=PACK)
            for g in range(GROUPS):
                old[(name, g)] = keep.tile([P, PACK, N], BF16, name="old_%s_%d" % (name, g))
                nc.sync.dma_start(out=old[(name, g)][:], in_=rows[g])

        y_rows = out_0.rearrange("(g p t) n -> g p t n", p=P, t=PACK)
        y_words = out_1.rearrange("g p n t -> g p (n t)").bitcast(I32)
        y_scales = out_2.bitcast(I32)
        scale_out = keep.tile([P, N], U8, name="scale_out", align_bytes=64)

        planes, mixed, codes, scales = {}, {}, {}, {}
        banks, average, bounded, updated, rounded, words = {}, {}, {}, {}, {}, {}
        passes_done = {u: 0 for u in range(len(units))}

        def widen(i, vector_part):
            name, c, k = pieces[i]
            if i not in planes:
                planes[i] = work.tile([P, PACK, PIECE], BF16, name="planes")
            for t in range(PACK):
                if ((i, t) in on_vector) != vector_part:
                    continue
                src = raw[pieces[i]][:, t, :].bitcast(FP8)
                col = token_scale[name][:, k, t : t + 1]
                if vector_part:
                    nc.vector.tensor_scalar(
                        out=planes[i][:, t, :], in0=src, scalar1=col, scalar2=None, op0=ALU.mult
                    )
                else:
                    nc.scalar.activation(out=planes[i][:, t, :], in_=src, func=ACT.Copy, scale=col)

        def interleave(i):
            mixed[i] = work.tile([P, PIECE * PACK], BF16, name="mixed", align_bytes=64)
            if pieces[i][0] == "x":
                dst = mixed[i][:].rearrange("p (r a e t) -> p a t e r", r=PACK, e=2, t=PACK)
                src = planes[i][:].rearrange("p t (a e r) -> p a t e r", e=2, r=PACK)
            else:
                dst = mixed[i][:].rearrange("p (a e t) -> p a t e", e=4, t=PACK)
                src = planes[i][:].rearrange("p t (a e) -> p a t e", e=4)
            if i == len(pieces) - 1:
                nc.scalar.copy(out=dst, in_=src)
            else:
                nc.vector.tensor_copy(out=dst, in_=src)

        def quantize(i):
            codes[pieces[i]] = keep.tile([P, PIECE], U32, name="codes_%d" % i, align_bytes=64)
            scales[pieces[i]] = keep.tile([P, PIECE], U8, name="scales_%d" % i, align_bytes=64)
            nc.vector.quantize_mx(
                out=codes[pieces[i]][:].bitcast(FP8X4), scales=scales[pieces[i]][:], in_=mixed[i][:]
            )

        def multiply_ready():
            for k in range(PASSES):
                for u, (g, c, b) in enumerate(units):
                    if passes_done[u] != k or (u >= OPEN_UNITS and u - OPEN_UNITS not in average):
                        continue
                    if ("x", g, k) not in codes or ("d", c, k) not in codes:
                        continue
                    for j in range(2):
                        if k == 0:
                            banks[(u, j)] = psum.tile([P, PIECE], F32, name="bank")
                        r = 2 * b + j
                        m_cols = slice(r * P, (r + 1) * P)
                        nc.tensor.matmul_mx(
                            out=banks[(u, j)][:],
                            lhsT=codes[("x", g, k)][:, m_cols].bitcast(FP8X4),
                            lhsT_scale=scales[("x", g, k)][:, m_cols],
                            rhs=codes[("d", c, k)][:].bitcast(FP8X4),
                            rhs_scale=scales[("d", c, k)][:],
                            start=(k == 0),
                            stop=(k == PASSES - 1),
                        )
                    passes_done[u] = k + 1

        def momentum(u):
            g, c, b = units[u]
            cols = slice(c * PIECE, (c + 1) * PIECE)
            average[u] = work.tile([P, 2, PIECE], F32, name="average")
            for j in range(2):
                nc.vector.scalar_tensor_tensor(
                    out=average[u][:, j, :],
                    in0=old[("v", g)][:, 2 * b + j, cols],
                    scalar=MU / (1.0 - MU),
                    in1=banks[(u, j)][:],
                    op0=ALU.mult,
                    op1=ALU.add,
                )

        def bound(u):
            bounded[u] = work.tile([P, 2, PIECE], F32, name="bounded")
            nc.scalar.activation(
                out=bounded[u][:], in_=average[u][:], func=ACT.Tanh, scale=-(1.0 - MU)
            )

        def update(u):
            g, c, b = units[u]
            cols = slice(c * PIECE, (c + 1) * PIECE)
            if b == 0:
                updated[(g, c)] = work.tile([P, PACK, PIECE], F32, name="updated")
            for j in range(2):
                r = 2 * b + j
                nc.vector.scalar_tensor_tensor(
                    out=updated[(g, c)][:, r, :],
                    in0=bounded[u][:, j, :],
                    scalar=step_size[:, g, r : r + 1],
                    in1=old[("w", g)][:, r, cols],
                    op0=ALU.mult,
                    op1=ALU.add,
                )
            nc.sync.dma_start(
                out=y_rows[g][:, 2 * b : 2 * b + 2, cols],
                in_=updated[(g, c)][:, 2 * b : 2 * b + 2, :],
            )

        def round_y(u):
            g, c, b = units[u]
            rounded[u] = work.tile([P, UNIT * PACK], BF16, name="rounded", align_bytes=64)
            dst = rounded[u][:].rearrange("p (a e r) -> p a r e", e=4, r=PACK)
            src = updated[(g, c)][:, :, b * UNIT : (b + 1) * UNIT].rearrange("p r (a e) -> p a r e", e=4)
            if u == len(units) - 2:
                nc.vector.tensor_copy(out=dst, in_=src)
            else:
                nc.scalar.copy(out=dst, in_=src)

        def quantize_y(u):
            g, c, b = units[u]
            cols = slice(c * PIECE + b * UNIT, c * PIECE + (b + 1) * UNIT)
            if b == 0:
                words[(g, c)] = outs.tile([P, PIECE], U32, name="words_out", align_bytes=64)
            nc.vector.quantize_mx(
                out=words[(g, c)][:, b * UNIT : (b + 1) * UNIT].bitcast(FP8X4),
                scales=scale_out[4 * g : P, cols],
                in_=rounded[u][:],
            )
            if b == 1:
                nc.sync.dma_start(
                    out=y_words[g][:, c * PIECE : (c + 1) * PIECE],
                    in_=words[(g, c)][:].bitcast(I32),
                )
            if u == len(units) - 1:
                for q in range(4):
                    nc.scalar.dma_start(
                        out=y_scales[:, 4 * q : 4 * q + 4, :],
                        in_=scale_out[32 * q : 32 * q + 4 * GROUPS, :].bitcast(I32),
                    )

        def piece_stage(stage, i, *more):
            if 0 <= i < len(pieces):
                stage(i, *more)

        def unit_stage(stage, u):
            if 0 <= u < len(units):
                stage(u)

        for step in range(-1, FIRST_UNIT_STEP + len(units) + 5):
            u = step - FIRST_UNIT_STEP
            unit_stage(momentum, u)
            multiply_ready()
            piece_stage(widen, step + 1, True)
            if step != len(pieces) - 1:
                piece_stage(interleave, step)
            unit_stage(update, u - 2)
            if u - 4 == len(units) - 2:
                round_y(u - 4)
            unit_stage(quantize_y, u - 5)
            piece_stage(quantize, step - 1)
            multiply_ready()
            unit_stage(bound, u - 1)
            if u - 4 != len(units) - 2:
                unit_stage(round_y, u - 4)
            if step == len(pieces) - 1:
                interleave(step)
            piece_stage(widen, step + 1, False)
